import numpy as np
CORES = [0,1,2,3]
N = 4
def setup_inputs(rng):
    return {"x": rng.standard_normal((N, 128, 8), dtype=np.float32)}
def reference(x):
    s = (x.sum(axis=0, dtype=np.float64) / N).astype(x.dtype)
    b = 8 // N
    return {"y": np.stack([s[:, r * b:(r + 1) * b] for r in range(N)])}

from concourse.bass import DstId, RemoteDMATransfer
from concourse.mybir import AluOpType

B = 2

SCRATCH = {
    "xs": ("sbuf", [128, 8], "float32"),
    "land": ("sbuf", [128, 8], "float32"),
    "t4": ("sbuf", [128, 4], "float32"),
    "t2": ("sbuf", [128, 2], "float32"),
    "quarter": ("sbuf", [128, 2], "float32"),
    "out": ("sbuf", [128, 2], "float32"),
}
SEMAPHORES = ["loaded", "read", "arrived", "stored", "v"]

ENGINES = 4


def rank_program(g, core, T, topo):
    rank = T.rank_of(core)
    if rank is None:
        return
    n = len(T.cores)
    mine = slice(rank * B, (rank + 1) * B)

    g.vector.memset(T.quarter[:], 1.0 / n).then_inc(T.sem.v, 1)

    g.dma_start(T.xs[:], T.x[:]).then_inc(T.sem.loaded, 16)
    g.dma_start(T.land[:, mine], T.x[:, mine]).then_inc(T.sem.loaded, 16)
    g.wait_ge(T.sem.loaded, 32)

    transfers = []
    for k, j in enumerate(p for p in range(n) if p != rank):
        rid, pid = topo.addr(T.cores[j])[:2]
        transfers.append(RemoteDMATransfer(
            dst_ids=[DstId(rid=rid, pnc=pid)],
            dma_engine_mask=((1 << ENGINES) - 1) << (ENGINES * k),
            remote_sem=T.sem.arrived,
            src=T.xs[:, j * B:(j + 1) * B],
            dst=T.land[:, mine],
        ))
    g.remote_dma_fused(transfers, local_sem=T.sem.read)

    ve = g.vector
    ve.wait_ge(T.sem.loaded, 32)
    ve.wait_ge(T.sem.arrived, ENGINES * (n - 1))
    ve.tensor_tensor(T.t4[:], T.land[:, 0:4], T.land[:, 4:8], AluOpType.add).then_inc(T.sem.v, 1)
    ve.wait_ge(T.sem.v, 2)
    ve.tensor_tensor(T.t2[:], T.t4[:, 0:2], T.t4[:, 2:4], AluOpType.add).then_inc(T.sem.v, 1)
    ve.wait_ge(T.sem.v, 3)
    ve.tensor_tensor(T.out[:], T.t2[:], T.quarter[:], AluOpType.mult).then_inc(T.sem.v, 1)

    g.wait_ge(T.sem.v, 4)
    g.dma_start(T.y[:], T.out[:]).then_inc(T.sem.stored, 16)
    g.wait_ge(T.sem.read, ENGINES * (n - 1))
    g.wait_ge(T.sem.stored, 16)
